import numpy as np
import ml_dtypes


def mxq(x, axis, fmt="e4m3"):
    dtype, down = {"e4m3": (ml_dtypes.float8_e4m3fn, 7), "e5m2": (ml_dtypes.float8_e5m2, 14)}[fmt]
    v = np.moveaxis(np.asarray(x, np.float32).astype(ml_dtypes.bfloat16).astype(np.float64), axis, -1)
    blocks = v.reshape(v.shape[:-1] + (-1, 32))
    amax = np.abs(blocks).max(-1, keepdims=True)
    byte = np.maximum(np.where(amax > 0, np.frexp(amax)[1] - 1 + 127, 0) - down, 1)
    scale = np.exp2(byte - 127.0)
    codes = (blocks / scale).astype(np.float32).astype(dtype).astype(np.float64)
    return np.moveaxis((codes * scale).reshape(v.shape), -1, axis)


WIDE = False


def mx_kscale(k):
    if not WIDE:
        return np.ones(k)
    levels = np.array([10, -10, 5, -5, 0])
    if k % 512:
        return np.exp2(np.random.permutation(np.resize(levels, k // 32))).repeat(32)
    a = np.empty((k // 512, 16))
    for p in range(k // 512):
        a[p, :8] = np.random.permutation(np.resize(levels, 8))
        for g in range(8):
            far = levels[np.abs(levels - a[p, g]) >= 10]
            a[p, g + 8] = far[np.random.randint(len(far))]
    return np.exp2(a.ravel()).repeat(32)


def f64(x):
    return np.asarray(x).astype(np.float64)


def striped(idx):
    return np.tile(idx.reshape(-1, 16).T, (8, 1)).astype(np.uint16)


def unstriped(offs):
    return offs[:16].T.reshape(-1).astype(np.int64)


E2M1 = np.array([0.0, 0.5, 1.0, 1.5, 2.0, 3.0, 4.0, 6.0, -0.0, -0.5, -1.0, -1.5, -2.0, -3.0, -4.0, -6.0])


def pack_weight(w, fmt):
    k, n = w.shape
    w = f64(np.asarray(w, np.float32).astype(ml_dtypes.bfloat16)).reshape(k // 32, 32, n)
    amax = np.abs(w).max(1)
    if fmt == "e4m3":
        byte = np.frexp(amax)[1] - 1 + 127 - 7
    else:
        mant, ex = np.frexp(amax / 6.0)
        byte = np.where(mant > 0.5, ex, ex - 1) + 127
    byte = np.clip(np.where(amax > 0, byte, 1), 1, 254)
    scaled = (w * np.exp2(127.0 - byte)[:, None, :]).reshape(k, n).astype(np.float32)
    by_word = np.ascontiguousarray(scaled.reshape(k // 512, 128, 4, n).transpose(0, 1, 3, 2))
    if fmt == "e4m3":
        words = by_word.astype(ml_dtypes.float8_e4m3fn).view(np.uint8)
    else:
        c = by_word.astype(ml_dtypes.float4_e2m1fn).view(np.uint8) & 0xF
        words = (c[..., 0::2] | (c[..., 1::2] << 4)).reshape(k // 512, 128, 2 * n)
    return np.ascontiguousarray(words), np.ascontiguousarray(byte.astype(np.uint8).reshape(k // 512, 16, n))


def unpack_weight(words, scales, fmt):
    g, _, n = scales.shape
    words = np.ascontiguousarray(words).reshape(g, 128, n, -1)
    if fmt == "e4m3":
        vals = words.view(ml_dtypes.float8_e4m3fn).astype(np.float64)
    else:
        nib = np.empty((g, 128, n, 4), np.uint8)
        nib[..., 0::2] = words & 0xF
        nib[..., 1::2] = words >> 4
        vals = E2M1[nib]
    vals = vals * np.repeat(np.exp2(scales.astype(np.float64) - 127.0), 8, axis=1)[..., None]
    return vals.transpose(0, 1, 3, 2).reshape(g * 512, n)


def gelu(v):
    return 0.5 * v * (1.0 + np.tanh(np.sqrt(2.0 / np.pi) * (v + 0.044715 * v**3)))


KL, KV, K, H, T, S, T2, P = 1024, 1024, 2048, 1024, 2048, 512, 1024, 512

def setup_inputs():
    n = np.random.standard_normal
    s = mx_kscale(K)[:, None]
    u = mx_kscale(H)[:, None]
    d = {}
    d["tab_words"], d["tab_scales"] = pack_weight(n((K, T)) * s, "e4m3")
    d["offs"] = striped(np.random.permutation(T)[:S])
    d["w1"] = (1.6 * n((KL, H)) / K**0.5 / s[:KL] * u.T).astype(np.float32)
    d["w4_words"], d["w4_scales"] = pack_weight(1.6 * n((KV, H)) / K**0.5 / s[KL:] * u.T, "e2m1")
    d["base"] = (0.5 * np.exp(0.6 * n(H)) * u[:, 0]**2).astype(np.float32)
    d["wgs"] = np.exp(0.3 * n((128, S))).astype(np.float32)
    d["page0"] = (n((H, T2)) * u).astype(np.float32)
    d["offs2"] = striped(np.random.permutation(T2)[:S])
    d["offs3"] = striped(np.random.permutation(T2)[:P])
    d["limit"] = ((0.6 + 1.2 * n((H, P))) * u).astype(np.float32)
    d["wref"] = (n(H) / H**0.5 / u[:, 0]**2).astype(np.float32)
    d["least"] = (0.2 * np.exp(0.7 * n(T2))).astype(np.float32)
    return d

def reference(tab_words, tab_scales, offs, w1, w4_words, w4_scales, base, wgs, page0, offs2, offs3, limit, wref, least):
    v = unpack_weight(tab_words, tab_scales, "e4m3")[:, unstriped(offs)]
    w4 = unpack_weight(w4_words, w4_scales, "e2m1")
    y = mxq(f64(w1), 0, "e4m3").T @ v[:KL] + w4.T @ v[KL:]
    h = np.sqrt(np.square(y) + f64(base)[:, None])
    page = f64(page0).copy()
    page[:, unstriped(offs2)] = np.tile(f64(wgs), (H // 128, 1)) * h
    x = np.minimum(page[:, unstriped(offs3)], f64(limit)) * f64(wref)[:, None]
    e = mxq(page, 0, "e4m3").T @ mxq(x, 0, "e4m3")
    return np.sqrt(np.maximum(e, f64(least)[:, None]))

@@ -1,0 +1,258 @@
+from contextlib import ExitStack
+
+import concourse.mybir as mybir
+
+F32 = mybir.dt.float32
+BF16 = mybir.dt.bfloat16
+I32 = mybir.dt.int32
+U32 = mybir.dt.uint32
+U16 = mybir.dt.uint16
+U8 = mybir.dt.uint8
+FP8X4 = mybir.dt.float8_e4m3fn_x4
+FP4X4 = mybir.dt.float4_e2m1fn_x4
+ALU = mybir.AluOpType
+ACT = mybir.ActivationFunctionType
+
+KL, KV, H, T, S, T2, NREF = 1024, 1024, 1024, 2048, 512, 1024, 512
+FLOPS = 2 * (KL + KV) * H * S + 2 * H * T2 * NREF
+
+P = 128
+PACK = 4
+K_PASS = P * PACK
+HALVES = H // K_PASS
+
+
+def tile_list_stamper_noise_page_kernel(
+    tc, tab_words, tab_scales, offs, w1, w4_words, w4_scales, base, wgs, page0, offs2, offs3, limit, wref, least, out
+):
+    nc = tc.nc
+    with ExitStack() as ctx:
+        keep = ctx.enter_context(tc.tile_pool(name="keep", bufs=1))
+        ring = ctx.enter_context(tc.tile_pool(name="ring", bufs=2))
+        psum = ctx.enter_context(tc.psum_pool(name="psum", bufs=1))
+
+        list1 = keep.tile([P, S // 16], U16, name="list1")
+        list2 = keep.tile([P, S // 16], U16, name="list2")
+        list3 = keep.tile([P, NREF // 16], U16, name="list3")
+
+        tab_sc = keep.tile([P, 2 * T], U8, name="tab_sc", align_bytes=64)
+        w4_sc_raw = keep.tile([P, 2 * H], U8, name="w4_sc_raw", align_bytes=64)
+        nc.gpsimd.memset(w4_sc_raw[:].bitcast(I32), 0)
+        nc.vector.memset(tab_sc[:].bitcast(I32), 0)
+
+        warm = keep.tile([P, 8], F32, name="warm")
+        warm2 = keep.tile([P, 8], F32, name="warm2")
+        nc.vector.memset(warm[:], 1.0)
+        nc.scalar.activation(warm2[:], warm[:], ACT.Sqrt)
+
+        w4_raw = keep.tile([P, 2 * 2 * H], U8, name="w4_raw", align_bytes=64)
+        tab = [keep.tile([P, T], U32, name=f"tab{a}", align_bytes=64) for a in range(4)]
+        page = [keep.tile([P, T2], F32, name=f"page{i}", align_bytes=64) for i in range(HALVES * PACK)]
+        gains = [keep.tile([P, 2, S], F32, name=f"gains{u}", align_bytes=64) for u in range(2)]
+        base_t = keep.tile([P, HALVES, PACK], F32, name="base_t")
+        wref_t = keep.tile([P, HALVES, PACK], F32, name="wref_t")
+        least_t = keep.tile([P, T2 // P], F32, name="least_t")
+        w1_raw = {}
+        lim = {}
+
+        def load_tab(a):
+            nc.sync.dma_start(out=tab[a][:].bitcast(I32), in_=tab_words[a].rearrange("p n t -> p (n t)").bitcast(I32))
+
+        def load_w1(half, a):
+            raw = ring.tile([P, PACK, K_PASS], F32, name="w1_raw", tag="staged", bufs=4, align_bytes=64)
+            rows = w1[a * K_PASS : (a + 1) * K_PASS, half * K_PASS : (half + 1) * K_PASS]
+            nc.sync.dma_start(out=raw[:], in_=rows.rearrange("(p j) c -> p j c", j=PACK))
+            w1_raw[half, a] = raw
+
+        def load_gains(u):
+            rows = wgs.rearrange("(q t) j -> q t j", t=PACK)[:, 2 * u : 2 * u + 2, :]
+            for rep in (0, 2, 1, 3):
+                nc.sync.dma_start(out=gains[u][32 * rep : 32 * rep + 32, :, :], in_=rows)
+
+        def load_page(i):
+            half, t = divmod(i, PACK)
+            rows = page0[half * K_PASS : (half + 1) * K_PASS, :].rearrange("(p t) m -> p t m", t=PACK)
+            nc.sync.dma_start(out=page[i][:], in_=rows[:, t, :])
+
+        def load_limit(half):
+            tile = ring.tile([P, PACK, NREF], F32, name="lim", tag="staged", bufs=4, align_bytes=64)
+            rows = limit[half * K_PASS : (half + 1) * K_PASS, :].rearrange("(p t) j -> p t j", t=PACK)
+            nc.sync.dma_start(out=tile[:], in_=rows)
+            lim[half] = tile
+
+        def load_w4_scales(q):
+            nc.gpsimd.dma_start(
+                out=w4_sc_raw[32 * q : 32 * q + 4, :].rearrange("r (a c) -> r a c", a=2).bitcast(I32),
+                in_=w4_scales[:, 4 * q : 4 * q + 4, :].rearrange("a r c -> r a c").bitcast(I32),
+            )
+
+        def load_tab_scales(q, first_pass, first_row):
+            rows = slice(32 * q + first_row, 32 * q + first_row + 4)
+            nc.sync.dma_start(
+                out=tab_sc[rows, :].rearrange("r (a c) -> r a c", a=2).bitcast(I32),
+                in_=tab_scales[first_pass : first_pass + 2, 4 * q : 4 * q + 4, :].rearrange("a r c -> r a c").bitcast(I32),
+            )
+
+        for q in range(4):
+            load_w4_scales(q)
+        load_tab(2)
+        nc.sync.dma_start(list1[:], offs)
+        nc.sync.dma_start(
+            out=w4_raw[:].rearrange("p (a c) -> p a c", a=2).bitcast(I32),
+            in_=w4_words.rearrange("a p c -> p a c").bitcast(I32),
+        )
+        for q in range(4):
+            load_tab_scales(q, 2, 0)
+        load_w1(0, 0)
+        for q in range(4):
+            load_tab_scales(q, 0, 4)
+        load_tab(3)
+        load_w1(0, 1)
+        load_tab(0)
+        nc.sync.dma_start(out=base_t[:], in_=base.rearrange("(a p t) -> p a t", p=P, t=PACK))
+        load_tab(1)
+        nc.sync.dma_start(list2[:], offs2)
+        load_gains(0)
+        load_page(0)
+        nc.sync.dma_start(list3[:], offs3)
+        nc.sync.dma_start(out=wref_t[:], in_=wref.rearrange("(a p t) -> p a t", p=P, t=PACK))
+        load_w1(1, 0)
+        load_w1(1, 1)
+        load_page(1)
+
+        w4_codes = keep.tile([P, 2 * 2 * H], U8, name="w4_codes", align_bytes=64)
+        w4_sc = keep.tile([P, 2 * H], U8, name="w4_sc", align_bytes=64)
+        for half in range(HALVES):
+            for a in range(2):
+                cols = slice((2 * a + half) * 2 * K_PASS, (2 * a + half + 1) * 2 * K_PASS)
+                nc.vector.tensor_copy(
+                    out=w4_codes[:, cols].rearrange("p (t g m b) -> p g t m b", t=PACK, m=8, b=2),
+                    in_=w4_raw[:, cols].rearrange("p (g m t b) -> p g t m b", t=PACK, m=8, b=2),
+                )
+        nc.vector.tensor_copy(
+            out=w4_sc[:].rearrange("p (s t g m) -> p s g t m", s=4, t=PACK, m=16),
+            in_=w4_sc_raw[:].rearrange("p (s g m t) -> p s g t m", s=4, t=PACK, m=16),
+        )
+
+        v_codes = [keep.tile([P, S], U32, name=f"v_codes{a}", align_bytes=64) for a in range(4)]
+        v_sc = [keep.tile([P, S], U8, name=f"v_sc{c}", align_bytes=64) for c in range(2)]
+        for c in range(2):
+            nc.vector.tensor_copy(out=v_sc[c][:], in_=tab_sc[:, c * T : (c + 1) * T].indirect(list1[:]))
+        for a in (2, 3, 0, 1):
+            nc.vector.tensor_copy(out=v_codes[a][:], in_=tab[a][:].indirect(list1[:]))
+
+        w1_codes = {}
+        w1_sc = {}
+        h = []
+
+        def quantize_w1(half, a):
+            grouped = ring.tile([P, PACK * K_PASS], BF16, name="w1_bf", align_bytes=64)
+            src = w1_raw[half, a][:].rearrange("p j (m t) -> p m t j", t=PACK)
+            dst = grouped[:].rearrange("p (t m j) -> p m t j", t=PACK, j=PACK)
+            for c in range(2):
+                nc.scalar.copy(out=dst[:, 64 * c : 64 * c + 64], in_=src[:, 64 * c : 64 * c + 64])
+            codes = keep.tile([P, K_PASS], U32, name=f"w1_codes{half}{a}", align_bytes=64)
+            sc = keep.tile([P, K_PASS], U8, name=f"w1_sc{half}{a}", align_bytes=64)
+            nc.vector.quantize_mx(out=codes[:].bitcast(FP8X4), scales=sc[:], in_=grouped[:])
+            w1_codes[half, a] = codes
+            w1_sc[half, a] = sc
+
+        def first_stage(i):
+            half, t = divmod(i, PACK)
+            y = psum.tile([P, S], F32, name=f"y{i}", tag=f"bank{t}")
+            for a in range(2):
+                col = (2 * a + half) * K_PASS + t * P
+                nc.tensor.matmul_mx(
+                    out=y[:],
+                    lhsT=w4_codes[:, 2 * col : 2 * col + 2 * P].bitcast(FP4X4),
+                    lhsT_scale=w4_sc[:, col : col + P],
+                    rhs=v_codes[2 + a][:].bitcast(FP8X4),
+                    rhs_scale=v_sc[a][:],
+                    start=(a == 0),
+                    stop=False,
+                )
+            for a in range(2):
+                nc.tensor.matmul_mx(
+                    out=y[:],
+                    lhsT=w1_codes[half, a][:, t * P : (t + 1) * P].bitcast(FP8X4),
+                    lhsT_scale=w1_sc[half, a][:, t * P : (t + 1) * P],
+                    rhs=v_codes[a][:].bitcast(FP8X4),
+                    rhs_scale=v_sc[a][4:P, :],
+                    start=False,
+                    stop=(a == 1),
+                )
+            sq = ring.tile([P, S], F32, name="sq")
+            nc.scalar.activation(sq[:], y[:], ACT.Square)
+            root = keep.tile([P, S], F32, name=f"h{i}")
+            nc.scalar.activation(root[:], sq[:], ACT.Sqrt, bias=base_t[:, half, t : t + 1])
+            h.append(root)
+
+        for half in range(HALVES):
+            for a in range(2):
+                quantize_w1(half, a)
+            for t in range(PACK):
+                first_stage(half * PACK + t)
+
+        load_limit(0)
+        load_gains(1)
+        load_page(2)
+        load_page(3)
+        load_page(4)
+        load_limit(1)
+        with nc.allow_non_contiguous_dma(reason="one least score a partition"):
+            nc.sync.dma_start(out=least_t[:], in_=least.rearrange("(b p) -> p b", p=P))
+        load_page(5)
+        load_page(6)
+        load_page(7)
+
+        scores = [psum.tile([P, NREF], F32, name=f"e{b}", tag=f"bank{b}") for b in range(T2 // P)]
+        for half in range(HALVES):
+            page_pairs = ring.tile([P, 2, T2, 2], BF16, name="page_pairs", bufs=1, align_bytes=64)
+            x_pairs = ring.tile([P, 2, NREF, 2], BF16, name="x_pairs", bufs=1, align_bytes=64)
+            for t in range(PACK):
+                i = half * PACK + t
+                nc.vector.tensor_tensor(page[i][:].indirect(list2[:]), h[i][:], gains[t // 2][:, t % 2, :], ALU.mult)
+                picked = ring.tile([P, NREF], F32, name="picked", bufs=4)
+                nc.vector.tensor_copy(out=picked[:], in_=page[i][:].indirect(list3[:]))
+                low = ring.tile([P, NREF], F32, name="low", bufs=3)
+                nc.vector.tensor_tensor(low[:], picked[:], lim[half][:, t, :], ALU.min)
+                nc.scalar.copy(out=page_pairs[:, t // 2, :, t % 2], in_=page[i][:])
+                nc.scalar.activation(x_pairs[:, t // 2, :, t % 2], low[:], ACT.Copy, scale=wref_t[:, half, t : t + 1])
+            x_bf = ring.tile([P, NREF * PACK], BF16, name="x_bf", bufs=1, align_bytes=64)
+            nc.scalar.copy(
+                out=x_bf[:].bitcast(F32).rearrange("p (j u) -> p j u", u=2),
+                in_=x_pairs[:].rearrange("p u j e -> p u (j e)").bitcast(F32).rearrange("p u j -> p j u"),
+            )
+            x_codes = ring.tile([P, NREF], U32, name="x_codes", align_bytes=64)
+            x_sc = ring.tile([P, NREF], U8, name="x_sc", align_bytes=64)
+            nc.vector.quantize_mx(out=x_codes[:].bitcast(FP8X4), scales=x_sc[:], in_=x_bf[:])
+            words = page_pairs[:].rearrange("p u m e -> p u (m e)").bitcast(F32)
+            for c in range(2):
+                cols = slice(c * 512, (c + 1) * 512)
+                page_bf = ring.tile([P, 512 * PACK], BF16, name="page_bf", align_bytes=64)
+                dst = page_bf[:].bitcast(F32).rearrange("p (m u) -> p m u", u=2)
+                src = words[:, :, cols].rearrange("p u m -> p m u")
+                if half == 0:
+                    nc.scalar.copy(out=dst, in_=src)
+                else:
+                    nc.vector.tensor_copy(out=dst, in_=src)
+                page_codes = ring.tile([P, 512], U32, name="page_codes", bufs=4, align_bytes=64)
+                page_sc = ring.tile([P, 512], U8, name="page_sc", bufs=4, align_bytes=64)
+                nc.vector.quantize_mx(out=page_codes[:].bitcast(FP8X4), scales=page_sc[:], in_=page_bf[:])
+                for b in range(4):
+                    nc.tensor.matmul_mx(
+                        out=scores[4 * c + b][:],
+                        lhsT=page_codes[:, b * P : (b + 1) * P].bitcast(FP8X4),
+                        lhsT_scale=page_sc[:, b * P : (b + 1) * P],
+                        rhs=x_codes[:].bitcast(FP8X4),
+                        rhs_scale=x_sc[:],
+                        start=(half == 0),
+                        stop=(half == HALVES - 1),
+                    )
+
+        for b in range(T2 // P):
+            floor = ring.tile([P, NREF], F32, name="floor", bufs=3)
+            nc.vector.tensor_scalar(floor[:], scores[b][:], least_t[:, b : b + 1], None, ALU.max)
+            result = ring.tile([P, NREF], F32, name="result", bufs=4)
+            nc.scalar.activation(result[:], floor[:], ACT.Sqrt)
+            nc.sync.dma_start(out=out[b * P : (b + 1) * P, :], in_=result[:])

@@ -45,9 +45,9 @@ def tile_list_stamper_noise_page_kernel(
         nc.vector.memset(warm[:], 1.0)
         nc.scalar.activation(warm2[:], warm[:], ACT.Sqrt)
 
-        w4_raw = keep.tile([P, 2 * 2 * H], U8, name="w4_raw", align_bytes=64)
+        w4_raw = [keep.tile([P, 2, H], U8, name=f"w4_raw{half}", align_bytes=64) for half in range(HALVES)]
         tab = [keep.tile([P, T], U32, name=f"tab{a}", align_bytes=64) for a in range(4)]
-        page = [keep.tile([P, T2], F32, name=f"page{i}", align_bytes=64) for i in range(HALVES * PACK)]
+        page = [keep.tile([P, T2], F32, name=f"page{i}", tag=f"page{i}", align_bytes=64) for i in range(HALVES * PACK)]
         gains = [keep.tile([P, 2, S], F32, name=f"gains{u}", align_bytes=64) for u in range(2)]
         base_t = keep.tile([P, HALVES, PACK], F32, name="base_t")
         wref_t = keep.tile([P, HALVES, PACK], F32, name="wref_t")
@@ -59,7 +59,7 @@ def tile_list_stamper_noise_page_kernel(
             nc.sync.dma_start(out=tab[a][:].bitcast(I32), in_=tab_words[a].rearrange("p n t -> p (n t)").bitcast(I32))
 
         def load_w1(half, a):
-            raw = ring.tile([P, PACK, K_PASS], F32, name="w1_raw", tag="staged", bufs=4, align_bytes=64)
+            raw = ring.tile([P, PACK, K_PASS], F32, name="w1_raw", tag=f"staged{half}{a}", bufs=1, align_bytes=64)
             rows = w1[a * K_PASS : (a + 1) * K_PASS, half * K_PASS : (half + 1) * K_PASS]
             nc.sync.dma_start(out=raw[:], in_=rows.rearrange("(p j) c -> p j c", j=PACK))
             w1_raw[half, a] = raw
@@ -75,13 +75,19 @@ def tile_list_stamper_noise_page_kernel(
             nc.sync.dma_start(out=page[i][:], in_=rows[:, t, :])
 
         def load_limit(half):
-            tile = ring.tile([P, PACK, NREF], F32, name="lim", tag="staged", bufs=4, align_bytes=64)
+            tile = ring.tile([P, PACK, NREF], F32, name="lim", tag=f"staged0{half}", bufs=1, align_bytes=64)
             rows = limit[half * K_PASS : (half + 1) * K_PASS, :].rearrange("(p t) j -> p t j", t=PACK)
             nc.sync.dma_start(out=tile[:], in_=rows)
             lim[half] = tile
 
+        def load_w4_words(half):
+            nc.sync.dma_start(
+                out=w4_raw[half][:].bitcast(I32),
+                in_=w4_words[:, :, half * H : (half + 1) * H].rearrange("a p c -> p a c").bitcast(I32),
+            )
+
         def load_w4_scales(q):
-            nc.gpsimd.dma_start(
+            nc.sync.dma_start(
                 out=w4_sc_raw[32 * q : 32 * q + 4, :].rearrange("r (a c) -> r a c", a=2).bitcast(I32),
                 in_=w4_scales[:, 4 * q : 4 * q + 4, :].rearrange("a r c -> r a c").bitcast(I32),
             )
@@ -93,41 +99,42 @@ def tile_list_stamper_noise_page_kernel(
                 in_=tab_scales[first_pass : first_pass + 2, 4 * q : 4 * q + 4, :].rearrange("a r c -> r a c").bitcast(I32),
             )
 
-        for q in range(4):
-            load_w4_scales(q)
         load_tab(2)
         nc.sync.dma_start(list1[:], offs)
-        nc.sync.dma_start(
-            out=w4_raw[:].rearrange("p (a c) -> p a c", a=2).bitcast(I32),
-            in_=w4_words.rearrange("a p c -> p a c").bitcast(I32),
-        )
+        load_w4_words(0)
         for q in range(4):
-            load_tab_scales(q, 2, 0)
+            load_w4_scales(q)
         load_w1(0, 0)
+        load_tab_scales(0, 2, 0)
+        load_tab_scales(1, 2, 0)
+        load_tab(3)
+        load_tab_scales(2, 2, 0)
+        load_tab_scales(3, 2, 0)
         for q in range(4):
             load_tab_scales(q, 0, 4)
-        load_tab(3)
         load_w1(0, 1)
         load_tab(0)
         nc.sync.dma_start(out=base_t[:], in_=base.rearrange("(a p t) -> p a t", p=P, t=PACK))
         load_tab(1)
+        load_w4_words(1)
         nc.sync.dma_start(list2[:], offs2)
         load_gains(0)
         load_page(0)
-        nc.sync.dma_start(list3[:], offs3)
-        nc.sync.dma_start(out=wref_t[:], in_=wref.rearrange("(a p t) -> p a t", p=P, t=PACK))
-        load_w1(1, 0)
-        load_w1(1, 1)
         load_page(1)
+        nc.sync.dma_start(list3[:], offs3)
+        load_w1(1, 0)
+        load_gains(1)
+        load_page(2)
+        load_w1(1, 1)
+        nc.sync.dma_start(out=wref_t[:], in_=wref.rearrange("(a p t) -> p a t", p=P, t=PACK))
 
-        w4_codes = keep.tile([P, 2 * 2 * H], U8, name="w4_codes", align_bytes=64)
+        w4_codes = [keep.tile([P, 2, H], U8, name=f"w4_codes{half}", align_bytes=64) for half in range(HALVES)]
         w4_sc = keep.tile([P, 2 * H], U8, name="w4_sc", align_bytes=64)
         for half in range(HALVES):
             for a in range(2):
-                cols = slice((2 * a + half) * 2 * K_PASS, (2 * a + half + 1) * 2 * K_PASS)
                 nc.vector.tensor_copy(
-                    out=w4_codes[:, cols].rearrange("p (t g m b) -> p g t m b", t=PACK, m=8, b=2),
-                    in_=w4_raw[:, cols].rearrange("p (g m t b) -> p g t m b", t=PACK, m=8, b=2),
+                    out=w4_codes[half][:, a, :].rearrange("p (t g m b) -> p g t m b", t=PACK, m=8, b=2),
+                    in_=w4_raw[half][:, a, :].rearrange("p (g m t b) -> p g t m b", t=PACK, m=8, b=2),
                 )
         nc.vector.tensor_copy(
             out=w4_sc[:].rearrange("p (s t g m) -> p s g t m", s=4, t=PACK, m=16),
@@ -145,15 +152,20 @@ def tile_list_stamper_noise_page_kernel(
         w1_sc = {}
         h = []
 
-        def quantize_w1(half, a):
+        w1_bf = {}
+
+        def round_w1(half, a):
             grouped = ring.tile([P, PACK * K_PASS], BF16, name="w1_bf", align_bytes=64)
             src = w1_raw[half, a][:].rearrange("p j (m t) -> p m t j", t=PACK)
             dst = grouped[:].rearrange("p (t m j) -> p m t j", t=PACK, j=PACK)
             for c in range(2):
                 nc.scalar.copy(out=dst[:, 64 * c : 64 * c + 64], in_=src[:, 64 * c : 64 * c + 64])
+            w1_bf[half, a] = grouped
+
+        def quantize_w1(half, a):
             codes = keep.tile([P, K_PASS], U32, name=f"w1_codes{half}{a}", align_bytes=64)
             sc = keep.tile([P, K_PASS], U8, name=f"w1_sc{half}{a}", align_bytes=64)
-            nc.vector.quantize_mx(out=codes[:].bitcast(FP8X4), scales=sc[:], in_=grouped[:])
+            nc.vector.quantize_mx(out=codes[:].bitcast(FP8X4), scales=sc[:], in_=w1_bf[half, a][:])
             w1_codes[half, a] = codes
             w1_sc[half, a] = sc
 
@@ -164,7 +176,7 @@ def tile_list_stamper_noise_page_kernel(
                 col = (2 * a + half) * K_PASS + t * P
                 nc.tensor.matmul_mx(
                     out=y[:],
-                    lhsT=w4_codes[:, 2 * col : 2 * col + 2 * P].bitcast(FP4X4),
+                    lhsT=w4_codes[half][:, a, 2 * t * P : 2 * (t + 1) * P].bitcast(FP4X4),
                     lhsT_scale=w4_sc[:, col : col + P],
                     rhs=v_codes[2 + a][:].bitcast(FP8X4),
                     rhs_scale=v_sc[a][:],
@@ -183,19 +195,18 @@ def tile_list_stamper_noise_page_kernel(
                 )
             sq = ring.tile([P, S], F32, name="sq")
             nc.scalar.activation(sq[:], y[:], ACT.Square)
-            root = keep.tile([P, S], F32, name=f"h{i}")
+            root = keep.tile([P, S], F32, name=f"h{i}", tag=f"slot{i}", align_bytes=64)
             nc.scalar.activation(root[:], sq[:], ACT.Sqrt, bias=base_t[:, half, t : t + 1])
             h.append(root)
 
         for half in range(HALVES):
             for a in range(2):
+                round_w1(half, a)
                 quantize_w1(half, a)
             for t in range(PACK):
                 first_stage(half * PACK + t)
 
         load_limit(0)
-        load_gains(1)
-        load_page(2)
         load_page(3)
         load_page(4)
         load_limit(1)
@@ -206,53 +217,85 @@ def tile_list_stamper_noise_page_kernel(
         load_page(7)
 
         scores = [psum.tile([P, NREF], F32, name=f"e{b}", tag=f"bank{b}") for b in range(T2 // P)]
-        for half in range(HALVES):
-            page_pairs = ring.tile([P, 2, T2, 2], BF16, name="page_pairs", bufs=1, align_bytes=64)
-            x_pairs = ring.tile([P, 2, NREF, 2], BF16, name="x_pairs", bufs=1, align_bytes=64)
-            for t in range(PACK):
-                i = half * PACK + t
-                nc.vector.tensor_tensor(page[i][:].indirect(list2[:]), h[i][:], gains[t // 2][:, t % 2, :], ALU.mult)
-                picked = ring.tile([P, NREF], F32, name="picked", bufs=4)
-                nc.vector.tensor_copy(out=picked[:], in_=page[i][:].indirect(list3[:]))
-                low = ring.tile([P, NREF], F32, name="low", bufs=3)
-                nc.vector.tensor_tensor(low[:], picked[:], lim[half][:, t, :], ALU.min)
-                nc.scalar.copy(out=page_pairs[:, t // 2, :, t % 2], in_=page[i][:])
-                nc.scalar.activation(x_pairs[:, t // 2, :, t % 2], low[:], ACT.Copy, scale=wref_t[:, half, t : t + 1])
-            x_bf = ring.tile([P, NREF * PACK], BF16, name="x_bf", bufs=1, align_bytes=64)
-            nc.scalar.copy(
-                out=x_bf[:].bitcast(F32).rearrange("p (j u) -> p j u", u=2),
-                in_=x_pairs[:].rearrange("p u j e -> p u (j e)").bitcast(F32).rearrange("p u j -> p j u"),
-            )
-            x_codes = ring.tile([P, NREF], U32, name="x_codes", align_bytes=64)
-            x_sc = ring.tile([P, NREF], U8, name="x_sc", align_bytes=64)
-            nc.vector.quantize_mx(out=x_codes[:].bitcast(FP8X4), scales=x_sc[:], in_=x_bf[:])
-            words = page_pairs[:].rearrange("p u m e -> p u (m e)").bitcast(F32)
+        n_tiles = HALVES * PACK
+        page_pairs = {}
+        x_pairs = {}
+        picked = {}
+        low = {}
+        page_q = {}
+
+        def scatter(i):
+            half, t = divmod(i, PACK)
+            nc.vector.tensor_tensor(page[i][:].indirect(list2[:]), h[i][:], gains[t // 2][:, t % 2, :], ALU.mult)
+            if t == 0:
+                page_pairs[half] = ring.tile([P, 2, T2, 2], BF16, name="page_pairs", tag=f"staged1{1 - half}", bufs=1, align_bytes=64)
+            nc.scalar.copy(out=page_pairs[half][:, t // 2, :, t % 2], in_=page[i][:])
+
+        def gather(i):
+            nc.vector.tensor_copy(out=picked[i], in_=page[i][:].indirect(list3[:]))
+
+        def clip(i):
+            half, t = divmod(i, PACK)
+            nc.vector.tensor_tensor(low[i], picked[i], lim[half][:, t, :], ALU.min)
+            if t == 0:
+                x_pairs[half] = ring.tile([P, 2, NREF, 2], BF16, name="x_pairs", bufs=1, align_bytes=64)
+            nc.scalar.activation(x_pairs[half][:, t // 2, :, t % 2], low[i], ACT.Copy, scale=wref_t[:, half, t : t + 1])
+
+        def quantize_page(half):
+            words = page_pairs[half][:].rearrange("p u m e -> p u (m e)").bitcast(F32)
             for c in range(2):
-                cols = slice(c * 512, (c + 1) * 512)
                 page_bf = ring.tile([P, 512 * PACK], BF16, name="page_bf", align_bytes=64)
-                dst = page_bf[:].bitcast(F32).rearrange("p (m u) -> p m u", u=2)
-                src = words[:, :, cols].rearrange("p u m -> p m u")
-                if half == 0:
-                    nc.scalar.copy(out=dst, in_=src)
-                else:
-                    nc.vector.tensor_copy(out=dst, in_=src)
+                nc.scalar.copy(
+                    out=page_bf[:].bitcast(F32).rearrange("p (m u) -> p m u", u=2),
+                    in_=words[:, :, c * 512 : (c + 1) * 512].rearrange("p u m -> p m u"),
+                )
                 page_codes = ring.tile([P, 512], U32, name="page_codes", bufs=4, align_bytes=64)
                 page_sc = ring.tile([P, 512], U8, name="page_sc", bufs=4, align_bytes=64)
                 nc.vector.quantize_mx(out=page_codes[:].bitcast(FP8X4), scales=page_sc[:], in_=page_bf[:])
-                for b in range(4):
-                    nc.tensor.matmul_mx(
-                        out=scores[4 * c + b][:],
-                        lhsT=page_codes[:, b * P : (b + 1) * P].bitcast(FP8X4),
-                        lhsT_scale=page_sc[:, b * P : (b + 1) * P],
-                        rhs=x_codes[:].bitcast(FP8X4),
-                        rhs_scale=x_sc[:],
-                        start=(half == 0),
-                        stop=(half == HALVES - 1),
-                    )
+                page_q[half, c] = (page_codes, page_sc)
+
+        def second_stage(half):
+            x_bf = ring.tile([P, NREF * PACK], BF16, name="x_bf", bufs=1, align_bytes=64)
+            dst = x_bf[:].bitcast(F32).rearrange("p (j u) -> p j u", u=2)
+            src = x_pairs[half][:].rearrange("p u j e -> p u (j e)").bitcast(F32).rearrange("p u j -> p j u")
+            if half == 0:
+                nc.scalar.copy(out=dst, in_=src)
+            else:
+                nc.vector.tensor_copy(out=dst, in_=src)
+            x_codes = ring.tile([P, NREF], U32, name="x_codes", align_bytes=64)
+            x_sc = ring.tile([P, NREF], U8, name="x_sc", align_bytes=64)
+            nc.vector.quantize_mx(out=x_codes[:].bitcast(FP8X4), scales=x_sc[:], in_=x_bf[:])
+            for b in range(T2 // P):
+                page_codes, page_sc = page_q[half, b // 4]
+                cols = slice((b % 4) * P, (b % 4 + 1) * P)
+                nc.tensor.matmul_mx(
+                    out=scores[b][:],
+                    lhsT=page_codes[:, cols].bitcast(FP8X4),
+                    lhsT_scale=page_sc[:, cols],
+                    rhs=x_codes[:].bitcast(FP8X4),
+                    rhs_scale=x_sc[:],
+                    start=(half == 0),
+                    stop=(half == HALVES - 1),
+                )
+
+        for step in range(n_tiles + 2):
+            if step < n_tiles:
+                scatter(step)
+            if step >= 1:
+                after = keep.tile([P, 2, NREF], F32, name=f"after{step}", tag=f"slot{step % n_tiles}", align_bytes=64)
+                picked[step - 1] = after[:, 0, :]
+                low[step - 2] = after[:, 1, :]
+            if step >= 2:
+                clip(step - 2)
+            if 1 <= step <= n_tiles:
+                gather(step - 1)
+            if step % PACK == PACK - 1:
+                quantize_page(step // PACK)
+            if step >= 2 and (step - 2) % PACK == PACK - 1:
+                second_stage((step - 2) // PACK)
 
         for b in range(T2 // P):
-            floor = ring.tile([P, NREF], F32, name="floor", bufs=3)
-            nc.vector.tensor_scalar(floor[:], scores[b][:], least_t[:, b : b + 1], None, ALU.max)
-            result = ring.tile([P, NREF], F32, name="result", bufs=4)
-            nc.scalar.activation(result[:], floor[:], ACT.Sqrt)
-            nc.sync.dma_start(out=out[b * P : (b + 1) * P, :], in_=result[:])
+            last = keep.tile([P, 2, NREF], F32, name=f"last{b}", tag=f"page{b}", align_bytes=64)
+            nc.vector.tensor_scalar(last[:, 0, :], scores[b][:], least_t[:, b : b + 1], None, ALU.max)
+            nc.scalar.activation(last[:, 1, :], last[:, 0, :], ACT.Sqrt)
+            nc.sync.dma_start(out=out[b * P : (b + 1) * P, :], in_=last[:, 1, :])

@@ -48,7 +48,9 @@ def tile_list_stamper_noise_page_kernel(
         w4_raw = [keep.tile([P, 2, H], U8, name=f"w4_raw{half}", align_bytes=64) for half in range(HALVES)]
         tab = [keep.tile([P, T], U32, name=f"tab{a}", align_bytes=64) for a in range(4)]
         page = [keep.tile([P, T2], F32, name=f"page{i}", tag=f"page{i}", align_bytes=64) for i in range(HALVES * PACK)]
-        gains = [keep.tile([P, 2, S], F32, name=f"gains{u}", align_bytes=64) for u in range(2)]
+        gain_slots = ((0,), (1,), (2, 3))
+        gain_tiles = [keep.tile([P, len(g), S], F32, name=f"gains{g[0]}", align_bytes=64) for g in gain_slots]
+        gains = [gain_tiles[u][:, n, :] for u, g in enumerate(gain_slots) for n in range(len(g))]
         base_t = keep.tile([P, HALVES, PACK], F32, name="base_t")
         wref_t = keep.tile([P, HALVES, PACK], F32, name="wref_t")
         least_t = keep.tile([P, T2 // P], F32, name="least_t")
@@ -65,9 +67,9 @@ def tile_list_stamper_noise_page_kernel(
             w1_raw[half, a] = raw
 
         def load_gains(u):
-            rows = wgs.rearrange("(q t) j -> q t j", t=PACK)[:, 2 * u : 2 * u + 2, :]
+            rows = wgs.rearrange("(q t) j -> q t j", t=PACK)[:, gain_slots[u][0] : gain_slots[u][-1] + 1, :]
             for rep in (0, 2, 1, 3):
-                nc.sync.dma_start(out=gains[u][32 * rep : 32 * rep + 32, :, :], in_=rows)
+                nc.sync.dma_start(out=gain_tiles[u][32 * rep : 32 * rep + 32, :, :], in_=rows)
 
         def load_page(i):
             half, t = divmod(i, PACK)
@@ -86,17 +88,16 @@ def tile_list_stamper_noise_page_kernel(
                 in_=w4_words[:, :, half * H : (half + 1) * H].rearrange("a p c -> p a c").bitcast(I32),
             )
 
-        def load_w4_scales(q):
+        def load_w4_scales(r):
             nc.sync.dma_start(
-                out=w4_sc_raw[32 * q : 32 * q + 4, :].rearrange("r (a c) -> r a c", a=2).bitcast(I32),
-                in_=w4_scales[:, 4 * q : 4 * q + 4, :].rearrange("a r c -> r a c").bitcast(I32),
+                out=w4_sc_raw[r:P:32, :].rearrange("q (a c) -> q a c", a=2).bitcast(I32),
+                in_=w4_scales[:, r:16:4, :].rearrange("a q c -> q a c").bitcast(I32),
             )
 
-        def load_tab_scales(q, first_pass, first_row):
-            rows = slice(32 * q + first_row, 32 * q + first_row + 4)
+        def load_tab_scales(r, first_pass, first_row):
             nc.sync.dma_start(
-                out=tab_sc[rows, :].rearrange("r (a c) -> r a c", a=2).bitcast(I32),
-                in_=tab_scales[first_pass : first_pass + 2, 4 * q : 4 * q + 4, :].rearrange("a r c -> r a c").bitcast(I32),
+                out=tab_sc[first_row + r : P : 32, :].rearrange("q (a c) -> q a c", a=2).bitcast(I32),
+                in_=tab_scales[first_pass : first_pass + 2, r:16:4, :].rearrange("a q c -> q a c").bitcast(I32),
             )
 
         load_tab(2)
@@ -106,24 +107,24 @@ def tile_list_stamper_noise_page_kernel(
             load_w4_scales(q)
         load_w1(0, 0)
         load_tab_scales(0, 2, 0)
-        load_tab_scales(1, 2, 0)
+        load_tab_scales(0, 0, 4)
         load_tab(3)
-        load_tab_scales(2, 2, 0)
-        load_tab_scales(3, 2, 0)
-        for q in range(4):
-            load_tab_scales(q, 0, 4)
+        for r in range(1, 4):
+            load_tab_scales(r, 2, 0)
+            load_tab_scales(r, 0, 4)
         load_w1(0, 1)
         load_tab(0)
-        nc.sync.dma_start(out=base_t[:], in_=base.rearrange("(a p t) -> p a t", p=P, t=PACK))
         load_tab(1)
-        load_w4_words(1)
+        nc.sync.dma_start(out=base_t[:], in_=base.rearrange("(a p t) -> p a t", p=P, t=PACK))
         nc.sync.dma_start(list2[:], offs2)
-        load_gains(0)
         load_page(0)
+        load_w4_words(1)
+        load_gains(0)
+        load_gains(1)
         load_page(1)
         nc.sync.dma_start(list3[:], offs3)
         load_w1(1, 0)
-        load_gains(1)
+        load_gains(2)
         load_page(2)
         load_w1(1, 1)
         nc.sync.dma_start(out=wref_t[:], in_=wref.rearrange("(a p t) -> p a t", p=P, t=PACK))
@@ -145,8 +146,12 @@ def tile_list_stamper_noise_page_kernel(
         v_sc = [keep.tile([P, S], U8, name=f"v_sc{c}", align_bytes=64) for c in range(2)]
         for c in range(2):
             nc.vector.tensor_copy(out=v_sc[c][:], in_=tab_sc[:, c * T : (c + 1) * T].indirect(list1[:]))
-        for a in (2, 3, 0, 1):
+        for a in (2, 3, 0):
             nc.vector.tensor_copy(out=v_codes[a][:], in_=tab[a][:].indirect(list1[:]))
+        for c in range(2):
+            nc.vector.tensor_copy(
+                out=v_codes[1][:, c * 256 : (c + 1) * 256], in_=tab[1][:].indirect(list1[:, c * 16 : (c + 1) * 16])
+            )
 
         w1_codes = {}
         w1_sc = {}
@@ -169,35 +174,59 @@ def tile_list_stamper_noise_page_kernel(
             w1_codes[half, a] = codes
             w1_sc[half, a] = sc
 
-        def first_stage(i):
+        def w1_pass(y, i, a, cols, start, stop):
             half, t = divmod(i, PACK)
-            y = psum.tile([P, S], F32, name=f"y{i}", tag=f"bank{t}")
-            for a in range(2):
-                col = (2 * a + half) * K_PASS + t * P
-                nc.tensor.matmul_mx(
-                    out=y[:],
-                    lhsT=w4_codes[half][:, a, 2 * t * P : 2 * (t + 1) * P].bitcast(FP4X4),
-                    lhsT_scale=w4_sc[:, col : col + P],
-                    rhs=v_codes[2 + a][:].bitcast(FP8X4),
-                    rhs_scale=v_sc[a][:],
-                    start=(a == 0),
-                    stop=False,
-                )
-            for a in range(2):
-                nc.tensor.matmul_mx(
-                    out=y[:],
-                    lhsT=w1_codes[half, a][:, t * P : (t + 1) * P].bitcast(FP8X4),
-                    lhsT_scale=w1_sc[half, a][:, t * P : (t + 1) * P],
-                    rhs=v_codes[a][:].bitcast(FP8X4),
-                    rhs_scale=v_sc[a][4:P, :],
-                    start=False,
-                    stop=(a == 1),
-                )
+            nc.tensor.matmul_mx(
+                out=y,
+                lhsT=w1_codes[half, a][:, t * P : (t + 1) * P].bitcast(FP8X4),
+                lhsT_scale=w1_sc[half, a][:, t * P : (t + 1) * P],
+                rhs=v_codes[a][:, cols].bitcast(FP8X4),
+                rhs_scale=v_sc[a][4:P, cols],
+                start=start,
+                stop=stop,
+            )
+
+        def w4_pass(y, i, a, cols, start):
+            half, t = divmod(i, PACK)
+            col = (2 * a + half) * K_PASS + t * P
+            nc.tensor.matmul_mx(
+                out=y,
+                lhsT=w4_codes[half][:, a, 2 * t * P : 2 * (t + 1) * P].bitcast(FP4X4),
+                lhsT_scale=w4_sc[:, col : col + P],
+                rhs=v_codes[2 + a][:, cols].bitcast(FP8X4),
+                rhs_scale=v_sc[a][:, cols],
+                start=start,
+                stop=False,
+            )
+
+        def noise(y, i, cols, root):
+            half, t = divmod(i, PACK)
             sq = ring.tile([P, S], F32, name="sq")
-            nc.scalar.activation(sq[:], y[:], ACT.Square)
+            nc.scalar.activation(sq[:, cols], y, ACT.Square)
+            nc.scalar.activation(root[:, cols], sq[:, cols], ACT.Sqrt, bias=base_t[:, half, t : t + 1])
+
+        def first_stage(i):
             root = keep.tile([P, S], F32, name=f"h{i}", tag=f"slot{i}", align_bytes=64)
-            nc.scalar.activation(root[:], sq[:], ACT.Sqrt, bias=base_t[:, half, t : t + 1])
             h.append(root)
+            if i == 0:
+                for c in range(2):
+                    y = psum.tile([P, 256], F32, name=f"y0{c}", tag=f"bank{4 * c}")
+                    cols = slice(c * 256, (c + 1) * 256)
+                    w1_pass(y[:], i, 0, cols, True, False)
+                    for a in range(2):
+                        for n in range(2):
+                            first = c * 256 + n * P
+                            w4_pass(y[:, n * P : (n + 1) * P], i, a, slice(first, first + P), False)
+                    w1_pass(y[:], i, 1, cols, False, True)
+                    noise(y[:], i, cols, root)
+            else:
+                y = psum.tile([P, S], F32, name=f"y{i}", tag=f"bank{i % PACK}")
+                cols = slice(0, S)
+                for a in range(2):
+                    w4_pass(y[:], i, a, cols, a == 0)
+                for a in range(2):
+                    w1_pass(y[:], i, a, cols, False, a == 1)
+                noise(y[:], i, cols, root)
 
         for half in range(HALVES):
             for a in range(2):
@@ -226,7 +255,12 @@ def tile_list_stamper_noise_page_kernel(
 
         def scatter(i):
             half, t = divmod(i, PACK)
-            nc.vector.tensor_tensor(page[i][:].indirect(list2[:]), h[i][:], gains[t // 2][:, t % 2, :], ALU.mult)
+            pieces = 2 if i == 0 else 1
+            for c in range(pieces):
+                n = S // pieces
+                cols = slice(c * n, (c + 1) * n)
+                places = list2[:, c * n // 16 : (c + 1) * n // 16]
+                nc.vector.tensor_tensor(page[i][:].indirect(places), h[i][:, cols], gains[t][:, cols], ALU.mult)
             if t == 0:
                 page_pairs[half] = ring.tile([P, 2, T2, 2], BF16, name="page_pairs", tag=f"staged1{1 - half}", bufs=1, align_bytes=64)
             nc.scalar.copy(out=page_pairs[half][:, t // 2, :, t % 2], in_=page[i][:])

@@ -89,36 +89,37 @@ def tile_list_stamper_noise_page_kernel(
             )
 
         def load_w4_scales(r):
-            nc.sync.dma_start(
+            nc.gpsimd.dma_start(
                 out=w4_sc_raw[r:P:32, :].rearrange("q (a c) -> q a c", a=2).bitcast(I32),
                 in_=w4_scales[:, r:16:4, :].rearrange("a q c -> q a c").bitcast(I32),
             )
 
-        def load_tab_scales(r, first_pass, first_row):
-            nc.sync.dma_start(
+        def load_tab_scales(queue, r, first_pass, first_row):
+            queue.dma_start(
                 out=tab_sc[first_row + r : P : 32, :].rearrange("q (a c) -> q a c", a=2).bitcast(I32),
                 in_=tab_scales[first_pass : first_pass + 2, r:16:4, :].rearrange("a q c -> q a c").bitcast(I32),
             )
 
+        for r in range(4):
+            load_w4_scales(r)
+        for r in range(4):
+            load_tab_scales(nc.gpsimd, r, 0, 4)
         load_tab(2)
         nc.sync.dma_start(list1[:], offs)
         load_w4_words(0)
-        for q in range(4):
-            load_w4_scales(q)
+        load_tab_scales(nc.sync, 0, 2, 0)
+        load_tab_scales(nc.sync, 1, 2, 0)
         load_w1(0, 0)
-        load_tab_scales(0, 2, 0)
-        load_tab_scales(0, 0, 4)
-        load_tab(3)
-        for r in range(1, 4):
-            load_tab_scales(r, 2, 0)
-            load_tab_scales(r, 0, 4)
+        load_tab_scales(nc.sync, 2, 2, 0)
+        load_tab_scales(nc.sync, 3, 2, 0)
         load_w1(0, 1)
+        load_tab(3)
         load_tab(0)
         load_tab(1)
         nc.sync.dma_start(out=base_t[:], in_=base.rearrange("(a p t) -> p a t", p=P, t=PACK))
         nc.sync.dma_start(list2[:], offs2)
-        load_page(0)
         load_w4_words(1)
+        load_page(0)
         load_gains(0)
         load_gains(1)
         load_page(1)
@@ -201,7 +202,7 @@ def tile_list_stamper_noise_page_kernel(
 
         def noise(y, i, cols, root):
             half, t = divmod(i, PACK)
-            sq = ring.tile([P, S], F32, name="sq")
+            sq = ring.tile([P, S], F32, name="sq", tag="sq_first" if i == 0 else "sq", bufs=1 if i == 0 else 2)
             nc.scalar.activation(sq[:, cols], y, ACT.Square)
             nc.scalar.activation(root[:, cols], sq[:, cols], ACT.Sqrt, bias=base_t[:, half, t : t + 1])
 
@@ -212,12 +213,12 @@ def tile_list_stamper_noise_page_kernel(
                 for c in range(2):
                     y = psum.tile([P, 256], F32, name=f"y0{c}", tag=f"bank{4 * c}")
                     cols = slice(c * 256, (c + 1) * 256)
-                    w1_pass(y[:], i, 0, cols, True, False)
                     for a in range(2):
                         for n in range(2):
                             first = c * 256 + n * P
-                            w4_pass(y[:, n * P : (n + 1) * P], i, a, slice(first, first + P), False)
-                    w1_pass(y[:], i, 1, cols, False, True)
+                            w4_pass(y[:, n * P : (n + 1) * P], i, a, slice(first, first + P), a == 0 and n == 0)
+                    for a in range(2):
+                        w1_pass(y[:], i, a, cols, False, a == 1)
                     noise(y[:], i, cols, root)
             else:
                 y = psum.tile([P, S], F32, name=f"y{i}", tag=f"bank{i % PACK}")
@@ -275,9 +276,9 @@ def tile_list_stamper_noise_page_kernel(
                 x_pairs[half] = ring.tile([P, 2, NREF, 2], BF16, name="x_pairs", bufs=1, align_bytes=64)
             nc.scalar.activation(x_pairs[half][:, t // 2, :, t % 2], low[i], ACT.Copy, scale=wref_t[:, half, t : t + 1])
 
-        def quantize_page(half):
+        def quantize_page(half, chunks):
             words = page_pairs[half][:].rearrange("p u m e -> p u (m e)").bitcast(F32)
-            for c in range(2):
+            for c in chunks:
                 page_bf = ring.tile([P, 512 * PACK], BF16, name="page_bf", align_bytes=64)
                 nc.scalar.copy(
                     out=page_bf[:].bitcast(F32).rearrange("p (m u) -> p m u", u=2),
@@ -299,6 +300,7 @@ def tile_list_stamper_noise_page_kernel(
             x_codes = ring.tile([P, NREF], U32, name="x_codes", align_bytes=64)
             x_sc = ring.tile([P, NREF], U8, name="x_sc", align_bytes=64)
             nc.vector.quantize_mx(out=x_codes[:].bitcast(FP8X4), scales=x_sc[:], in_=x_bf[:])
+            quantize_page(half, (1,))
             for b in range(T2 // P):
                 page_codes, page_sc = page_q[half, b // 4]
                 cols = slice((b % 4) * P, (b % 4 + 1) * P)
@@ -324,7 +326,7 @@ def tile_list_stamper_noise_page_kernel(
             if 1 <= step <= n_tiles:
                 gather(step - 1)
             if step % PACK == PACK - 1:
-                quantize_page(step // PACK)
+                quantize_page(step // PACK, (0,))
             if step >= 2 and (step - 2) % PACK == PACK - 1:
                 second_stage((step - 2) // PACK)
 

from contextlib import ExitStack

import concourse.mybir as mybir

F32 = mybir.dt.float32
BF16 = mybir.dt.bfloat16
I32 = mybir.dt.int32
U32 = mybir.dt.uint32
U16 = mybir.dt.uint16
U8 = mybir.dt.uint8
FP8X4 = mybir.dt.float8_e4m3fn_x4
FP4X4 = mybir.dt.float4_e2m1fn_x4
ALU = mybir.AluOpType
ACT = mybir.ActivationFunctionType

KL, KV, H, T, S, T2, NREF = 1024, 1024, 1024, 2048, 512, 1024, 512
FLOPS = 2 * (KL + KV) * H * S + 2 * H * T2 * NREF

P = 128
PACK = 4
K_PASS = P * PACK
HALVES = H // K_PASS


def tile_list_stamper_noise_page_kernel(
    tc, tab_words, tab_scales, offs, w1, w4_words, w4_scales, base, wgs, page0, offs2, offs3, limit, wref, least, out
):
    nc = tc.nc
    with ExitStack() as ctx:
        keep = ctx.enter_context(tc.tile_pool(name="keep", bufs=1))
        ring = ctx.enter_context(tc.tile_pool(name="ring", bufs=2))
        psum = ctx.enter_context(tc.psum_pool(name="psum", bufs=1))

        list1 = keep.tile([P, S // 16], U16, name="list1")
        list2 = keep.tile([P, S // 16], U16, name="list2")
        list3 = keep.tile([P, NREF // 16], U16, name="list3")

        tab_sc = keep.tile([P, 2 * T], U8, name="tab_sc", align_bytes=64)
        w4_sc_raw = keep.tile([P, 2 * H], U8, name="w4_sc_raw", align_bytes=64)
        nc.gpsimd.memset(w4_sc_raw[:].bitcast(I32), 0)
        nc.vector.memset(tab_sc[:].bitcast(I32), 0)

        warm = keep.tile([P, 8], F32, name="warm")
        warm2 = keep.tile([P, 8], F32, name="warm2")
        nc.vector.memset(warm[:], 1.0)
        nc.scalar.activation(warm2[:], warm[:], ACT.Sqrt)

        w4_raw = [keep.tile([P, 2, H], U8, name=f"w4_raw{half}", align_bytes=64) for half in range(HALVES)]
        tab = [keep.tile([P, T], U32, name=f"tab{a}", align_bytes=64) for a in range(4)]
        page = [keep.tile([P, T2], F32, name=f"page{i}", tag=f"page{i}", align_bytes=64) for i in range(HALVES * PACK)]
        gain_slots = ((0,), (1,), (2, 3))
        gain_tiles = [keep.tile([P, len(g), S], F32, name=f"gains{g[0]}", align_bytes=64) for g in gain_slots]
        gains = [gain_tiles[u][:, n, :] for u, g in enumerate(gain_slots) for n in range(len(g))]
        base_t = keep.tile([P, HALVES, PACK], F32, name="base_t")
        wref_t = keep.tile([P, HALVES, PACK], F32, name="wref_t")
        least_t = keep.tile([P, T2 // P], F32, name="least_t")
        w1_raw = {}
        lim = {}

        def load_tab(a):
            nc.sync.dma_start(out=tab[a][:].bitcast(I32), in_=tab_words[a].rearrange("p n t -> p (n t)").bitcast(I32))

        def load_w1(half, a):
            raw = ring.tile([P, PACK, K_PASS], F32, name="w1_raw", tag=f"staged{half}{a}", bufs=1, align_bytes=64)
            rows = w1[a * K_PASS : (a + 1) * K_PASS, half * K_PASS : (half + 1) * K_PASS]
            nc.sync.dma_start(out=raw[:], in_=rows.rearrange("(p j) c -> p j c", j=PACK))
            w1_raw[half, a] = raw

        def load_gains(u):
            rows = wgs.rearrange("(q t) j -> q t j", t=PACK)[:, gain_slots[u][0] : gain_slots[u][-1] + 1, :]
            for rep in (0, 2, 1, 3):
                nc.sync.dma_start(out=gain_tiles[u][32 * rep : 32 * rep + 32, :, :], in_=rows)

        def load_page(i):
            half, t = divmod(i, PACK)
            rows = page0[half * K_PASS : (half + 1) * K_PASS, :].rearrange("(p t) m -> p t m", t=PACK)
            nc.sync.dma_start(out=page[i][:], in_=rows[:, t, :])

        def load_limit(half):
            tile = ring.tile([P, PACK, NREF], F32, name="lim", tag=f"staged0{half}", bufs=1, align_bytes=64)
            rows = limit[half * K_PASS : (half + 1) * K_PASS, :].rearrange("(p t) j -> p t j", t=PACK)
            nc.sync.dma_start(out=tile[:], in_=rows)
            lim[half] = tile

        def load_w4_words(half):
            nc.sync.dma_start(
                out=w4_raw[half][:].bitcast(I32),
                in_=w4_words[:, :, half * H : (half + 1) * H].rearrange("a p c -> p a c").bitcast(I32),
            )

        def load_w4_scales(r):
            nc.gpsimd.dma_start(
                out=w4_sc_raw[r:P:32, :].rearrange("q (a c) -> q a c", a=2).bitcast(I32),
                in_=w4_scales[:, r:16:4, :].rearrange("a q c -> q a c").bitcast(I32),
            )

        def load_tab_scales(queue, r, first_pass, first_row):
            queue.dma_start(
                out=tab_sc[first_row + r : P : 32, :].rearrange("q (a c) -> q a c", a=2).bitcast(I32),
                in_=tab_scales[first_pass : first_pass + 2, r:16:4, :].rearrange("a q c -> q a c").bitcast(I32),
            )

        for r in range(4):
            load_w4_scales(r)
        for r in range(4):
            load_tab_scales(nc.gpsimd, r, 0, 4)
        load_tab(2)
        nc.sync.dma_start(list1[:], offs)
        load_w4_words(0)
        load_tab_scales(nc.sync, 0, 2, 0)
        load_tab_scales(nc.sync, 1, 2, 0)
        load_w1(0, 0)
        load_tab_scales(nc.sync, 2, 2, 0)
        load_tab_scales(nc.sync, 3, 2, 0)
        load_w1(0, 1)
        load_tab(3)
        load_tab(0)
        load_tab(1)
        nc.sync.dma_start(out=base_t[:], in_=base.rearrange("(a p t) -> p a t", p=P, t=PACK))
        nc.sync.dma_start(list2[:], offs2)
        load_w4_words(1)
        load_page(0)
        load_gains(0)
        load_gains(1)
        load_page(1)
        nc.sync.dma_start(list3[:], offs3)
        load_w1(1, 0)
        load_gains(2)
        load_page(2)
        load_w1(1, 1)
        nc.sync.dma_start(out=wref_t[:], in_=wref.rearrange("(a p t) -> p a t", p=P, t=PACK))

        w4_codes = [keep.tile([P, 2, H], U8, name=f"w4_codes{half}", align_bytes=64) for half in range(HALVES)]
        w4_sc = keep.tile([P, 2 * H], U8, name="w4_sc", align_bytes=64)
        for half in range(HALVES):
            for a in range(2):
                nc.vector.tensor_copy(
                    out=w4_codes[half][:, a, :].rearrange("p (t g m b) -> p g t m b", t=PACK, m=8, b=2),
                    in_=w4_raw[half][:, a, :].rearrange("p (g m t b) -> p g t m b", t=PACK, m=8, b=2),
                )
        nc.vector.tensor_copy(
            out=w4_sc[:].rearrange("p (s t g m) -> p s g t m", s=4, t=PACK, m=16),
            in_=w4_sc_raw[:].rearrange("p (s g m t) -> p s g t m", s=4, t=PACK, m=16),
        )

        v_codes = [keep.tile([P, S], U32, name=f"v_codes{a}", align_bytes=64) for a in range(4)]
        v_sc = [keep.tile([P, S], U8, name=f"v_sc{c}", align_bytes=64) for c in range(2)]
        for c in range(2):
            nc.vector.tensor_copy(out=v_sc[c][:], in_=tab_sc[:, c * T : (c + 1) * T].indirect(list1[:]))
        for a in (2, 3, 0):
            nc.vector.tensor_copy(out=v_codes[a][:], in_=tab[a][:].indirect(list1[:]))
        for c in range(2):
            nc.vector.tensor_copy(
                out=v_codes[1][:, c * 256 : (c + 1) * 256], in_=tab[1][:].indirect(list1[:, c * 16 : (c + 1) * 16])
            )

        w1_codes = {}
        w1_sc = {}
        h = []

        w1_bf = {}

        def round_w1(half, a):
            grouped = ring.tile([P, PACK * K_PASS], BF16, name="w1_bf", align_bytes=64)
            src = w1_raw[half, a][:].rearrange("p j (m t) -> p m t j", t=PACK)
            dst = grouped[:].rearrange("p (t m j) -> p m t j", t=PACK, j=PACK)
            for c in range(2):
                nc.scalar.copy(out=dst[:, 64 * c : 64 * c + 64], in_=src[:, 64 * c : 64 * c + 64])
            w1_bf[half, a] = grouped

        def quantize_w1(half, a):
            codes = keep.tile([P, K_PASS], U32, name=f"w1_codes{half}{a}", align_bytes=64)
            sc = keep.tile([P, K_PASS], U8, name=f"w1_sc{half}{a}", align_bytes=64)
            nc.vector.quantize_mx(out=codes[:].bitcast(FP8X4), scales=sc[:], in_=w1_bf[half, a][:])
            w1_codes[half, a] = codes
            w1_sc[half, a] = sc

        def w1_pass(y, i, a, cols, start, stop):
            half, t = divmod(i, PACK)
            nc.tensor.matmul_mx(
                out=y,
                lhsT=w1_codes[half, a][:, t * P : (t + 1) * P].bitcast(FP8X4),
                lhsT_scale=w1_sc[half, a][:, t * P : (t + 1) * P],
                rhs=v_codes[a][:, cols].bitcast(FP8X4),
                rhs_scale=v_sc[a][4:P, cols],
                start=start,
                stop=stop,
            )

        def w4_pass(y, i, a, cols, start):
            half, t = divmod(i, PACK)
            col = (2 * a + half) * K_PASS + t * P
            nc.tensor.matmul_mx(
                out=y,
                lhsT=w4_codes[half][:, a, 2 * t * P : 2 * (t + 1) * P].bitcast(FP4X4),
                lhsT_scale=w4_sc[:, col : col + P],
                rhs=v_codes[2 + a][:, cols].bitcast(FP8X4),
                rhs_scale=v_sc[a][:, cols],
                start=start,
                stop=False,
            )

        def noise(y, i, cols, root):
            half, t = divmod(i, PACK)
            sq = ring.tile([P, S], F32, name="sq", tag="sq_first" if i == 0 else "sq", bufs=1 if i == 0 else 2)
            nc.scalar.activation(sq[:, cols], y, ACT.Square)
            nc.scalar.activation(root[:, cols], sq[:, cols], ACT.Sqrt, bias=base_t[:, half, t : t + 1])

        def first_stage(i):
            root = keep.tile([P, S], F32, name=f"h{i}", tag=f"slot{i}", align_bytes=64)
            h.append(root)
            if i == 0:
                for c in range(2):
                    y = psum.tile([P, 256], F32, name=f"y0{c}", tag=f"bank{4 * c}")
                    cols = slice(c * 256, (c + 1) * 256)
                    for a in range(2):
                        for n in range(2):
                            first = c * 256 + n * P
                            w4_pass(y[:, n * P : (n + 1) * P], i, a, slice(first, first + P), a == 0 and n == 0)
                    for a in range(2):
                        w1_pass(y[:], i, a, cols, False, a == 1)
                    noise(y[:], i, cols, root)
            else:
                y = psum.tile([P, S], F32, name=f"y{i}", tag=f"bank{i % PACK}")
                cols = slice(0, S)
                for a in range(2):
                    w4_pass(y[:], i, a, cols, a == 0)
                for a in range(2):
                    w1_pass(y[:], i, a, cols, False, a == 1)
                noise(y[:], i, cols, root)

        for half in range(HALVES):
            for a in range(2):
                round_w1(half, a)
                quantize_w1(half, a)
            for t in range(PACK):
                first_stage(half * PACK + t)

        load_limit(0)
        load_page(3)
        load_page(4)
        load_limit(1)
        with nc.allow_non_contiguous_dma(reason="one least score a partition"):
            nc.sync.dma_start(out=least_t[:], in_=least.rearrange("(b p) -> p b", p=P))
        load_page(5)
        load_page(6)
        load_page(7)

        scores = [psum.tile([P, NREF], F32, name=f"e{b}", tag=f"bank{b}") for b in range(T2 // P)]
        n_tiles = HALVES * PACK
        page_pairs = {}
        x_pairs = {}
        picked = {}
        low = {}
        page_q = {}

        def scatter(i):
            half, t = divmod(i, PACK)
            pieces = 2 if i == 0 else 1
            for c in range(pieces):
                n = S // pieces
                cols = slice(c * n, (c + 1) * n)
                places = list2[:, c * n // 16 : (c + 1) * n // 16]
                nc.vector.tensor_tensor(page[i][:].indirect(places), h[i][:, cols], gains[t][:, cols], ALU.mult)
            if t == 0:
                page_pairs[half] = ring.tile([P, 2, T2, 2], BF16, name="page_pairs", tag=f"staged1{1 - half}", bufs=1, align_bytes=64)
            nc.scalar.copy(out=page_pairs[half][:, t // 2, :, t % 2], in_=page[i][:])

        def gather(i):
            nc.vector.tensor_copy(out=picked[i], in_=page[i][:].indirect(list3[:]))

        def clip(i):
            half, t = divmod(i, PACK)
            nc.vector.tensor_tensor(low[i], picked[i], lim[half][:, t, :], ALU.min)
            if t == 0:
                x_pairs[half] = ring.tile([P, 2, NREF, 2], BF16, name="x_pairs", bufs=1, align_bytes=64)
            nc.scalar.activation(x_pairs[half][:, t // 2, :, t % 2], low[i], ACT.Copy, scale=wref_t[:, half, t : t + 1])

        def quantize_page(half, chunks):
            words = page_pairs[half][:].rearrange("p u m e -> p u (m e)").bitcast(F32)
            for c in chunks:
                page_bf = ring.tile([P, 512 * PACK], BF16, name="page_bf", align_bytes=64)
                nc.scalar.copy(
                    out=page_bf[:].bitcast(F32).rearrange("p (m u) -> p m u", u=2),
                    in_=words[:, :, c * 512 : (c + 1) * 512].rearrange("p u m -> p m u"),
                )
                page_codes = ring.tile([P, 512], U32, name="page_codes", bufs=4, align_bytes=64)
                page_sc = ring.tile([P, 512], U8, name="page_sc", bufs=4, align_bytes=64)
                nc.vector.quantize_mx(out=page_codes[:].bitcast(FP8X4), scales=page_sc[:], in_=page_bf[:])
                page_q[half, c] = (page_codes, page_sc)

        def second_stage(half):
            x_bf = ring.tile([P, NREF * PACK], BF16, name="x_bf", bufs=1, align_bytes=64)
            dst = x_bf[:].bitcast(F32).rearrange("p (j u) -> p j u", u=2)
            src = x_pairs[half][:].rearrange("p u j e -> p u (j e)").bitcast(F32).rearrange("p u j -> p j u")
            if half == 0:
                nc.scalar.copy(out=dst, in_=src)
            else:
                nc.vector.tensor_copy(out=dst, in_=src)
            x_codes = ring.tile([P, NREF], U32, name="x_codes", align_bytes=64)
            x_sc = ring.tile([P, NREF], U8, name="x_sc", align_bytes=64)
            nc.vector.quantize_mx(out=x_codes[:].bitcast(FP8X4), scales=x_sc[:], in_=x_bf[:])
            quantize_page(half, (1,))
            for b in range(T2 // P):
                page_codes, page_sc = page_q[half, b // 4]
                cols = slice((b % 4) * P, (b % 4 + 1) * P)
                nc.tensor.matmul_mx(
                    out=scores[b][:],
                    lhsT=page_codes[:, cols].bitcast(FP8X4),
                    lhsT_scale=page_sc[:, cols],
                    rhs=x_codes[:].bitcast(FP8X4),
                    rhs_scale=x_sc[:],
                    start=(half == 0),
                    stop=(half == HALVES - 1),
                )

        for step in range(n_tiles + 2):
            if step < n_tiles:
                scatter(step)
            if step >= 1:
                after = keep.tile([P, 2, NREF], F32, name=f"after{step}", tag=f"slot{step % n_tiles}", align_bytes=64)
                picked[step - 1] = after[:, 0, :]
                low[step - 2] = after[:, 1, :]
            if step >= 2:
                clip(step - 2)
            if 1 <= step <= n_tiles:
                gather(step - 1)
            if step % PACK == PACK - 1:
                quantize_page(step // PACK, (0,))
            if step >= 2 and (step - 2) % PACK == PACK - 1:
                second_stage((step - 2) // PACK)

        for b in range(T2 // P):
            last = keep.tile([P, 2, NREF], F32, name=f"last{b}", tag=f"page{b}", align_bytes=64)
            nc.vector.tensor_scalar(last[:, 0, :], scores[b][:], least_t[:, b : b + 1], None, ALU.max)
            nc.scalar.activation(last[:, 1, :], last[:, 0, :], ACT.Sqrt)
            nc.sync.dma_start(out=out[b * P : (b + 1) * P, :], in_=last[:, 1, :])
